import numpy as np
import ml_dtypes


def mxq(x, axis, fmt="e4m3"):
    dtype, down = {"e4m3": (ml_dtypes.float8_e4m3fn, 7), "e5m2": (ml_dtypes.float8_e5m2, 14)}[fmt]
    v = np.moveaxis(np.asarray(x, np.float32).astype(ml_dtypes.bfloat16).astype(np.float64), axis, -1)
    blocks = v.reshape(v.shape[:-1] + (-1, 32))
    amax = np.abs(blocks).max(-1, keepdims=True)
    byte = np.maximum(np.where(amax > 0, np.frexp(amax)[1] - 1 + 127, 0) - down, 1)
    scale = np.exp2(byte - 127.0)
    codes = (blocks / scale).astype(np.float32).astype(dtype).astype(np.float64)
    return np.moveaxis((codes * scale).reshape(v.shape), -1, axis)


WIDE = False


def mx_kscale(k):
    if not WIDE:
        return np.ones(k)
    levels = np.array([10, -10, 5, -5, 0])
    if k % 512:
        return np.exp2(np.random.permutation(np.resize(levels, k // 32))).repeat(32)
    a = np.empty((k // 512, 16))
    for p in range(k // 512):
        a[p, :8] = np.random.permutation(np.resize(levels, 8))
        for g in range(8):
            far = levels[np.abs(levels - a[p, g]) >= 10]
            a[p, g + 8] = far[np.random.randint(len(far))]
    return np.exp2(a.ravel()).repeat(32)


def f64(x):
    return np.asarray(x).astype(np.float64)


E2M1 = np.array([0.0, 0.5, 1.0, 1.5, 2.0, 3.0, 4.0, 6.0, -0.0, -0.5, -1.0, -1.5, -2.0, -3.0, -4.0, -6.0])


def pack_weight(w, fmt):
    k, n = w.shape
    w = f64(np.asarray(w, np.float32).astype(ml_dtypes.bfloat16)).reshape(k // 32, 32, n)
    amax = np.abs(w).max(1)
    if fmt == "e4m3":
        byte = np.frexp(amax)[1] - 1 + 127 - 7
    else:
        mant, ex = np.frexp(amax / 6.0)
        byte = np.where(mant > 0.5, ex, ex - 1) + 127
    byte = np.clip(np.where(amax > 0, byte, 1), 1, 254)
    scaled = (w * np.exp2(127.0 - byte)[:, None, :]).reshape(k, n).astype(np.float32)
    by_word = np.ascontiguousarray(scaled.reshape(k // 512, 128, 4, n).transpose(0, 1, 3, 2))
    if fmt == "e4m3":
        words = by_word.astype(ml_dtypes.float8_e4m3fn).view(np.uint8)
    else:
        c = by_word.astype(ml_dtypes.float4_e2m1fn).view(np.uint8) & 0xF
        words = (c[..., 0::2] | (c[..., 1::2] << 4)).reshape(k // 512, 128, 2 * n)
    return np.ascontiguousarray(words), np.ascontiguousarray(byte.astype(np.uint8).reshape(k // 512, 16, n))


def unpack_weight(words, scales, fmt):
    g, _, n = scales.shape
    words = np.ascontiguousarray(words).reshape(g, 128, n, -1)
    if fmt == "e4m3":
        vals = words.view(ml_dtypes.float8_e4m3fn).astype(np.float64)
    else:
        nib = np.empty((g, 128, n, 4), np.uint8)
        nib[..., 0::2] = words & 0xF
        nib[..., 1::2] = words >> 4
        vals = E2M1[nib]
    vals = vals * np.repeat(np.exp2(scales.astype(np.float64) - 127.0), 8, axis=1)[..., None]
    return vals.transpose(0, 1, 3, 2).reshape(g * 512, n)


O, K, R, M, T = 1024, 2560, 512, 2048, 512


def setup_inputs():
    n = np.random.standard_normal
    s = mx_kscale(K)[:, None]
    u = mx_kscale(R)[:, None]
    x = n((K, T)); x[:O] *= 6.0
    w = n((K, M)) / np.sqrt(K) / s; w[:O] /= 2.0
    p_w8 = pack_weight(w[:O], "e4m3")
    p_w4 = pack_weight(w[O:], "e2m1")
    p_up = pack_weight(n((R, M)) / np.sqrt(R) / u, "e2m1")
    return {
        "x": (x * s).astype(np.float32),
        "w8_words": p_w8[0],
        "w8_scales": p_w8[1],
        "w4_words": p_w4[0],
        "w4_scales": p_w4[1],
        "down": (0.3 * n((K, R)) / np.sqrt(K) / s * u.T).astype(np.float32),
        "up_words": p_up[0],
        "up_scales": p_up[1],
        "b": (0.3 * n(2048)).astype(np.float32),
    }


def reference(x, w8_words, w8_scales, w4_words, w4_scales, down, up_words, up_scales, b):
    x_ = mxq(f64(x), 0, "e4m3")
    w8_ = unpack_weight(w8_words, w8_scales, "e4m3")
    w4_ = unpack_weight(w4_words, w4_scales, "e2m1")
    down_ = mxq(f64(down), 0, "e4m3")
    up_ = unpack_weight(up_words, up_scales, "e2m1")
    h_ = mxq(down_.T @ x_, 0, "e4m3")
    y = w8_.T @ x_[:O] + w4_.T @ x_[O:] + up_.T @ h_
    return y + f64(b)[:, None]

@@ -1,0 +1,279 @@
+from contextlib import ExitStack
+
+import concourse.mybir as mybir
+from concourse.masks import make_identity
+
+O, K, R, M, T = 1024, 2560, 512, 2048, 512
+FLOPS = 2 * K * R * T + 2 * (K + R) * M * T
+
+F32 = mybir.dt.float32
+BF16 = mybir.dt.bfloat16
+I32 = mybir.dt.int32
+U32 = mybir.dt.uint32
+U8 = mybir.dt.uint8
+E4M3 = mybir.dt.float8_e4m3fn_x4
+E2M1 = mybir.dt.float4_e2m1fn_x4
+IDENT = mybir.ActivationFunctionType.Identity
+
+P = 128
+PACK = 4
+KP = 512
+NK = K // KP
+NO = O // KP
+NT = M // P
+SECTIONS = ((0, 512), (512, 1024), (1024, 2048))
+XV = 384
+
+
+def tile_mix_three_fm_bias_kernel(
+    tc, x, w8_words, w8_scales, w4_words, w4_scales, down, up_words, up_scales, b, out
+):
+    nc = tc.nc
+    with ExitStack() as ctx:
+        keep = ctx.enter_context(tc.tile_pool(name="keep", bufs=1))
+        group = ctx.enter_context(tc.tile_pool(name="group", bufs=2))
+        res = ctx.enter_context(tc.tile_pool(name="res", bufs=4))
+        psum = ctx.enter_context(tc.psum_pool(name="psum", bufs=1))
+        ctx.enter_context(tc.manual_schedule())
+
+        x_raw = [keep.tile([P, PACK, T], F32, name=f"x_raw{g}") for g in range(NK)]
+        d_raw = [keep.tile([P, PACK, R], F32, name=f"d_raw{g}") for g in range(NK)]
+        x_codes = [keep.tile([P, T], U32, name=f"x_codes{g}", align_bytes=64) for g in range(NK)]
+        x_scale = [keep.tile([P, T], U8, name=f"x_scale{g}", align_bytes=64) for g in range(NK)]
+        d_codes = [keep.tile([P, R], U32, name=f"d_codes{g}", align_bytes=64) for g in range(NK)]
+        d_scale = [keep.tile([P, R], U8, name=f"d_scale{g}", align_bytes=64) for g in range(NK)]
+        w8 = [keep.tile([P, NO, c1 - c0], U32, name=f"w8_{c0}", align_bytes=64) for c0, c1 in SECTIONS]
+        w4 = [keep.tile([P, NK - NO, 2 * (c1 - c0)], U8, name=f"w4_{c0}", align_bytes=64) for c0, c1 in SECTIONS]
+        w8s = [keep.tile([P, c1 - c0], U8, name=f"w8s_{c0}", align_bytes=64) for c0, c1 in ((0, 512), (512, 2048))]
+        w4s = [keep.tile([P, NK - NO, c1 - c0], U8, name=f"w4s_{c0}", align_bytes=64) for c0, c1 in SECTIONS]
+        up = keep.tile([P, 2 * M], U8, name="up", align_bytes=64)
+        ups = keep.tile([P, M], U8, name="ups", align_bytes=64)
+        b_rows = keep.tile([P, P], F32, name="b_rows")
+        ident = keep.tile([P, P], F32, name="ident")
+        b_col = keep.tile([P, NT], F32, name="b_col")
+        warm = keep.tile([P, 1], F32, name="warm")
+        h_rows = keep.tile([P, PACK, T], BF16, name="h_rows", align_bytes=64)
+        h_grp = keep.tile([P, T, PACK], BF16, name="h_grp", align_bytes=64)
+        h_codes = keep.tile([P, T], U32, name="h_codes", align_bytes=64)
+        h_scale = keep.tile([P, T], U8, name="h_scale", align_bytes=64)
+
+        nc.vector.memset(warm[:], 0.0)
+        for t in (w8s[0], w4s[0]):
+            flat = t[:] if len(t.shape) == 2 else t[:].rearrange("p a n -> p (a n)")
+            nc.vector.memset(flat.bitcast(I32), 0)
+        nc.gpsimd.memset(b_rows[:], 0.0)
+        make_identity(nc, ident[:])
+        nc.scalar.activation(out=warm[:], in_=warm[:], func=IDENT)
+        nc.scalar.dma_start(out=b_rows[0:NT, :], in_=b.rearrange("(g p) -> g p", p=P))
+        for t in (w8s[1], w4s[1], w4s[2], ups):
+            flat = t[:] if len(t.shape) == 2 else t[:].rearrange("p a n -> p (a n)")
+            nc.vector.memset(flat.bitcast(I32), 0)
+
+        w8_view = w8_words.rearrange("a p n i -> p a (n i)")
+        w4_view = w4_words.rearrange("a p n -> p a n")
+        w4s_view = w4_scales.rearrange("a q n -> q a n")
+
+        def load_x(g):
+            nc.sync.dma_start(out=x_raw[g][:], in_=x[KP * g : KP * (g + 1), :].rearrange("(p j) t -> p j t", j=PACK))
+
+        def load_d(g, c0=0, c1=R):
+            nc.sync.dma_start(
+                out=d_raw[g][:, :, c0:c1],
+                in_=down[KP * g : KP * (g + 1), c0:c1].rearrange("(p j) r -> p j r", j=PACK),
+            )
+
+        def load_w8(s):
+            c0, c1 = SECTIONS[s]
+            nc.sync.dma_start(out=w8[s][:].bitcast(I32), in_=w8_view[:, :, 4 * c0 : 4 * c1].bitcast(I32))
+
+        def load_w4(s):
+            c0, c1 = SECTIONS[s]
+            nc.sync.dma_start(out=w4[s][:].bitcast(I32), in_=w4_view[:, :, 2 * c0 : 2 * c1].bitcast(I32))
+
+        def load_w8s(eng, s):
+            c0, c1 = ((0, 512), (512, 2048))[s]
+            for q in range(4):
+                eng.dma_start(
+                    out=w8s[s][32 * q : 32 * q + 8, :].bitcast(I32),
+                    in_=w8_scales[:, 4 * q : 4 * q + 4, c0:c1].bitcast(I32),
+                )
+
+        def load_w4s(eng, s):
+            c0, c1 = SECTIONS[s]
+            for q in range(4):
+                eng.dma_start(
+                    out=w4s[s][32 * q : 32 * q + 4, :, :].bitcast(I32),
+                    in_=w4s_view[4 * q : 4 * q + 4, :, c0:c1].bitcast(I32),
+                )
+
+        def load_ups(eng):
+            for q in range(4):
+                eng.dma_start(
+                    out=ups[32 * q : 32 * q + 4, :].bitcast(I32),
+                    in_=up_scales[0, 4 * q : 4 * q + 4, :].bitcast(I32),
+                )
+
+        load_w8s(nc.gpsimd, 0)
+        load_w4s(nc.gpsimd, 0)
+        for g in range(3):
+            load_x(g)
+            load_d(g)
+        load_x(3)
+        load_w8(0)
+        load_w4(0)
+        load_x(4)
+        load_d(3)
+        load_d(4, 0, R // 2)
+        load_d(4, R // 2, R)
+        load_w8s(nc.sync, 1)
+        load_w8(1)
+        load_w4s(nc.sync, 1)
+        load_w4(1)
+        load_ups(nc.sync)
+        nc.sync.dma_start(out=up[:].bitcast(I32), in_=up_words[0].bitcast(I32))
+        load_w4s(nc.sync, 2)
+        load_w8(2)
+        load_w4(2)
+
+        def quant_x(g):
+            grp = group.tile([P, T, PACK], BF16, name="x_grp", align_bytes=64)
+            for copy, c0, c1 in ((nc.vector.tensor_copy, 0, XV), (nc.scalar.copy, XV, T)):
+                copy(
+                    out=grp[:, c0:c1, :].rearrange("p (c i) j -> p c j i", i=4),
+                    in_=x_raw[g][:, :, c0:c1].rearrange("p j (c i) -> p c j i", i=4),
+                )
+            nc.vector.quantize_mx(
+                out=x_codes[g][:].bitcast(E4M3), scales=x_scale[g][:], in_=grp[:].rearrange("p t j -> p (t j)")
+            )
+
+        def spread_d(g, grp, m0, m1):
+            for copy, j0, j1 in ((nc.vector.tensor_copy, 0, 2), (nc.scalar.copy, 2, 4)):
+                copy(
+                    out=grp[:, j0:j1, m0:m1, :].rearrange("p t m j -> p m t j"),
+                    in_=d_raw[g][:].rearrange("p j (m t) -> p m t j", t=4)[:, m0:m1, j0:j1, :],
+                )
+
+        def quant_d(g, grp, j0, j1):
+            nc.vector.quantize_mx(
+                out=d_codes[g][:, P * j0 : P * j1].bitcast(E4M3),
+                scales=d_scale[g][:, P * j0 : P * j1],
+                in_=grp[:, j0:j1, :, :].rearrange("p t m j -> p (t m j)"),
+            )
+
+        def h_pass(g, j):
+            nc.tensor.matmul_mx(
+                out=h_acc[j][:],
+                lhsT=d_codes[g][:, P * j : P * (j + 1)].bitcast(E4M3),
+                lhsT_scale=d_scale[g][:, P * j : P * (j + 1)],
+                rhs=x_codes[g][:].bitcast(E4M3),
+                rhs_scale=x_scale[g][:],
+                start=(g == 0),
+                stop=(g == NK - 1),
+            )
+
+        def where(n):
+            c = P * n
+            s = 0 if c < 512 else (1 if c < 1024 else 2)
+            return s, c - SECTIONS[s][0]
+
+        def y_pass(n, g):
+            s, c = where(n)
+            if g < NO:
+                sc = w8s[0] if s == 0 else w8s[1]
+                cc = P * n if s == 0 else P * n - 512
+                lhsT = w8[s][:, g, c : c + P].bitcast(E4M3)
+                lscale = sc[4 * g : P, cc : cc + P]
+            else:
+                lhsT = w4[s][:, g - NO, 2 * c : 2 * (c + P)].bitcast(E2M1)
+                lscale = w4s[s][:, g - NO, c : c + P]
+            nc.tensor.matmul_mx(
+                out=y_acc[n][:], lhsT=lhsT, lhsT_scale=lscale,
+                rhs=x_codes[g][:].bitcast(E4M3), rhs_scale=x_scale[g][:],
+                start=(g == 0), stop=False,
+            )
+
+        def up_pass(n):
+            nc.tensor.matmul_mx(
+                out=y_acc[n][:],
+                lhsT=up[:, 2 * P * n : 2 * P * (n + 1)].bitcast(E2M1), lhsT_scale=ups[:, P * n : P * (n + 1)],
+                rhs=h_codes[:].bitcast(E4M3), rhs_scale=h_scale[:],
+                start=False, stop=True,
+            )
+
+        def finish(n):
+            o = res.tile([P, T], F32, name="o")
+            if n % 2 == 0:
+                nc.scalar.activation(out=o[:], in_=y_acc[n][:], func=IDENT, bias=b_col[:, n : n + 1])
+            else:
+                nc.vector.tensor_scalar_add(o[:], y_acc[n][:], b_col[:, n : n + 1])
+            nc.sync.dma_start(out=out[P * n : P * (n + 1), :], in_=o[:])
+
+        y_acc = {}
+
+        def open_bank(n):
+            y_acc[n] = psum.tile([P, T], F32, name=f"bank{n % 8}")
+
+        b_turn = psum.tile([P, P], F32, name="bank0")
+        nc.tensor.transpose(b_turn[:], b_rows[:], ident[:])
+        h_acc = [psum.tile([P, T], F32, name=f"bank{4 + j}") for j in range(PACK)]
+        for g in range(3):
+            quant_x(g)
+            if g == 0:
+                nc.scalar.copy(out=b_col[:], in_=b_turn[:, 0:NT])
+            d_grp = group.tile([P, PACK, P, PACK], BF16, name="d_grp", align_bytes=64)
+            spread_d(g, d_grp, 0, P)
+            quant_d(g, d_grp, 0, 4)
+            for j in range(PACK):
+                h_pass(g, j)
+        quant_x(3)
+        for n in range(4):
+            open_bank(n)
+        for g in range(4):
+            for n in range(4):
+                y_pass(n, g)
+        quant_x(4)
+        for n in range(4):
+            y_pass(n, 4)
+        d_grp = group.tile([P, PACK, P, PACK], BF16, name="d_grp", align_bytes=64)
+        spread_d(3, d_grp, 0, P)
+        quant_d(3, d_grp, 0, 4)
+        for j in range(PACK):
+            h_pass(3, j)
+        d_grp = group.tile([P, PACK, P, PACK], BF16, name="d_grp", align_bytes=64)
+        spread_d(4, d_grp, 0, P // 2)
+        spread_d(4, d_grp, P // 2, P)
+        quant_d(4, d_grp, 0, 2)
+        quant_d(4, d_grp, 2, 4)
+        for j in range(PACK):
+            h_pass(4, j)
+        for j in range(PACK):
+            copy = nc.vector.tensor_copy if j % 2 == 0 else nc.scalar.copy
+            copy(out=h_rows[:, j, :], in_=h_acc[j][:])
+        for n in range(4, 8):
+            open_bank(n)
+        for g in range(NO):
+            for n in range(4, 8):
+                y_pass(n, g)
+        for copy, c0, c1 in ((nc.vector.tensor_copy, 0, 320), (nc.scalar.copy, 320, T)):
+            copy(out=h_grp[:, c0:c1, :], in_=h_rows[:, :, c0:c1].rearrange("p j t -> p t j"))
+        nc.vector.quantize_mx(
+            out=h_codes[:].bitcast(E4M3), scales=h_scale[:], in_=h_grp[:].rearrange("p t j -> p (t j)")
+        )
+        for n in (4, 5):
+            for g in range(NO, NK):
+                y_pass(n, g)
+        for n in range(4):
+            up_pass(n)
+            finish(n)
+        for n in (6, 7):
+            for g in range(NO, NK):
+                y_pass(n, g)
+        for n in range(4, 8):
+            up_pass(n)
+            finish(n)
+        for n in range(8, NT):
+            open_bank(n)
+            for g in range(NK):
+                y_pass(n, g)
+            up_pass(n)
+            finish(n)

@@ -90,17 +90,17 @@ def tile_mix_three_fm_bias_kernel(
             c0, c1 = SECTIONS[s]
             nc.sync.dma_start(out=w4[s][:].bitcast(I32), in_=w4_view[:, :, 2 * c0 : 2 * c1].bitcast(I32))
 
-        def load_w8s(eng, s):
+        def load_w8s(eng, s, quads=(0, 1, 2, 3)):
             c0, c1 = ((0, 512), (512, 2048))[s]
-            for q in range(4):
+            for q in quads:
                 eng.dma_start(
                     out=w8s[s][32 * q : 32 * q + 8, :].bitcast(I32),
                     in_=w8_scales[:, 4 * q : 4 * q + 4, c0:c1].bitcast(I32),
                 )
 
-        def load_w4s(eng, s):
+        def load_w4s(eng, s, quads=(0, 1, 2, 3)):
             c0, c1 = SECTIONS[s]
-            for q in range(4):
+            for q in quads:
                 eng.dma_start(
                     out=w4s[s][32 * q : 32 * q + 4, :, :].bitcast(I32),
                     in_=w4s_view[4 * q : 4 * q + 4, :, c0:c1].bitcast(I32),
@@ -113,18 +113,19 @@ def tile_mix_three_fm_bias_kernel(
                     in_=up_scales[0, 4 * q : 4 * q + 4, :].bitcast(I32),
                 )
 
-        load_w8s(nc.gpsimd, 0)
-        load_w4s(nc.gpsimd, 0)
-        for g in range(3):
+        load_x(0)
+        load_d(0)
+        for g in (1, 2):
+            load_w8s(nc.sync, 0, (2 * g - 2, 2 * g - 1))
             load_x(g)
+            load_w4s(nc.sync, 0, (2 * g - 2, 2 * g - 1))
             load_d(g)
         load_x(3)
         load_w8(0)
         load_w4(0)
         load_x(4)
         load_d(3)
-        load_d(4, 0, R // 2)
-        load_d(4, R // 2, R)
+        load_d(4)
         load_w8s(nc.sync, 1)
         load_w8(1)
         load_w4s(nc.sync, 1)
@@ -176,7 +177,7 @@ def tile_mix_three_fm_bias_kernel(
             s = 0 if c < 512 else (1 if c < 1024 else 2)
             return s, c - SECTIONS[s][0]
 
-        def y_pass(n, g):
+        def y_pass(n, g, t0=0, t1=T):
             s, c = where(n)
             if g < NO:
                 sc = w8s[0] if s == 0 else w8s[1]
@@ -188,15 +189,15 @@ def tile_mix_three_fm_bias_kernel(
                 lscale = w4s[s][:, g - NO, c : c + P]
             nc.tensor.matmul_mx(
                 out=y_acc[n][:], lhsT=lhsT, lhsT_scale=lscale,
-                rhs=x_codes[g][:].bitcast(E4M3), rhs_scale=x_scale[g][:],
+                rhs=x_codes[g][:, t0:t1].bitcast(E4M3), rhs_scale=x_scale[g][:, t0:t1],
                 start=(g == 0), stop=False,
             )
 
-        def up_pass(n):
+        def up_pass(n, t0=0, t1=T):
             nc.tensor.matmul_mx(
                 out=y_acc[n][:],
                 lhsT=up[:, 2 * P * n : 2 * P * (n + 1)].bitcast(E2M1), lhsT_scale=ups[:, P * n : P * (n + 1)],
-                rhs=h_codes[:].bitcast(E4M3), rhs_scale=h_scale[:],
+                rhs=h_codes[:, t0:t1].bitcast(E4M3), rhs_scale=h_scale[:, t0:t1],
                 start=False, stop=True,
             )
 
@@ -240,10 +241,14 @@ def tile_mix_three_fm_bias_kernel(
         for j in range(PACK):
             h_pass(3, j)
         d_grp = group.tile([P, PACK, P, PACK], BF16, name="d_grp", align_bytes=64)
-        spread_d(4, d_grp, 0, P // 2)
-        spread_d(4, d_grp, P // 2, P)
-        quant_d(4, d_grp, 0, 2)
-        quant_d(4, d_grp, 2, 4)
+        for j in range(PACK):
+            copy = nc.vector.tensor_copy if j < 2 else nc.scalar.copy
+            copy(
+                out=d_grp[:, j, :, :],
+                in_=d_raw[4][:].rearrange("p j (m t) -> p m t j", t=4)[:, :, j, :],
+            )
+        for j in range(PACK):
+            quant_d(4, d_grp, j, j + 1)
         for j in range(PACK):
             h_pass(4, j)
         for j in range(PACK):
@@ -271,9 +276,24 @@ def tile_mix_three_fm_bias_kernel(
         for n in range(4, 8):
             up_pass(n)
             finish(n)
-        for n in range(8, NT):
+        for n in range(8, NT - 1):
             open_bank(n)
             for g in range(NK):
                 y_pass(n, g)
             up_pass(n)
             finish(n)
+        n = NT - 1
+        o = res.tile([P, T], F32, name="o")
+        for q in range(4):
+            y_acc[n] = psum.tile([P, P], F32, name=f"bank{q}")
+            for g in range(NK):
+                y_pass(n, g, P * q, P * (q + 1))
+            up_pass(n, P * q, P * (q + 1))
+            t0, t1 = P * q, P * (q + 1)
+            if q % 2 == 1:
+                nc.scalar.activation(out=o[:, t0:t1], in_=y_acc[n][:], func=IDENT, bias=b_col[:, n : n + 1])
+            else:
+                nc.vector.tensor_scalar_add(o[:, t0:t1], y_acc[n][:], b_col[:, n : n + 1])
+            if q > 0:
+                s0 = 0 if q == 1 else t0
+                nc.sync.dma_start(out=out[P * n : P * (n + 1), s0:t1], in_=o[:, s0:t1])

@@ -45,7 +45,7 @@ def tile_mix_three_fm_bias_kernel(
         w8 = [keep.tile([P, NO, c1 - c0], U32, name=f"w8_{c0}", align_bytes=64) for c0, c1 in SECTIONS]
         w4 = [keep.tile([P, NK - NO, 2 * (c1 - c0)], U8, name=f"w4_{c0}", align_bytes=64) for c0, c1 in SECTIONS]
         w8s = [keep.tile([P, c1 - c0], U8, name=f"w8s_{c0}", align_bytes=64) for c0, c1 in ((0, 512), (512, 2048))]
-        w4s = [keep.tile([P, NK - NO, c1 - c0], U8, name=f"w4s_{c0}", align_bytes=64) for c0, c1 in SECTIONS]
+        w4s = [keep.tile([P, NK - NO, c1 - c0], U8, name=f"w4s_{c0}", align_bytes=64) for c0, c1 in ((0, 512), (512, 2048))]
         up = keep.tile([P, 2 * M], U8, name="up", align_bytes=64)
         ups = keep.tile([P, M], U8, name="ups", align_bytes=64)
         b_rows = keep.tile([P, P], F32, name="b_rows")
@@ -65,7 +65,7 @@ def tile_mix_three_fm_bias_kernel(
         make_identity(nc, ident[:])
         nc.scalar.activation(out=warm[:], in_=warm[:], func=IDENT)
         nc.scalar.dma_start(out=b_rows[0:NT, :], in_=b.rearrange("(g p) -> g p", p=P))
-        for t in (w8s[1], w4s[1], w4s[2], ups):
+        for t in (w8s[1], w4s[1], ups):
             flat = t[:] if len(t.shape) == 2 else t[:].rearrange("p a n -> p (a n)")
             nc.vector.memset(flat.bitcast(I32), 0)
 
@@ -74,12 +74,15 @@ def tile_mix_three_fm_bias_kernel(
         w4s_view = w4_scales.rearrange("a q n -> q a n")
 
         def load_x(g):
-            nc.sync.dma_start(out=x_raw[g][:], in_=x[KP * g : KP * (g + 1), :].rearrange("(p j) t -> p j t", j=PACK))
-
-        def load_d(g, c0=0, c1=R):
             nc.sync.dma_start(
-                out=d_raw[g][:, :, c0:c1],
-                in_=down[KP * g : KP * (g + 1), c0:c1].rearrange("(p j) r -> p j r", j=PACK),
+                out=x_raw[g][:].rearrange("p j t -> p (j t)"),
+                in_=x[KP * g : KP * (g + 1), :].rearrange("(p j) t -> p (j t)", j=PACK),
+            )
+
+        def load_d(g):
+            nc.sync.dma_start(
+                out=d_raw[g][:].rearrange("p j r -> p (j r)"),
+                in_=down[KP * g : KP * (g + 1), :].rearrange("(p j) r -> p (j r)", j=PACK),
             )
 
         def load_w8(s):
@@ -99,7 +102,7 @@ def tile_mix_three_fm_bias_kernel(
                 )
 
         def load_w4s(eng, s, quads=(0, 1, 2, 3)):
-            c0, c1 = SECTIONS[s]
+            c0, c1 = ((0, 512), (512, 2048))[s]
             for q in quads:
                 eng.dma_start(
                     out=w4s[s][32 * q : 32 * q + 4, :, :].bitcast(I32),
@@ -120,19 +123,18 @@ def tile_mix_three_fm_bias_kernel(
             load_x(g)
             load_w4s(nc.sync, 0, (2 * g - 2, 2 * g - 1))
             load_d(g)
-        load_x(3)
         load_w8(0)
         load_w4(0)
+        load_x(3)
         load_x(4)
         load_d(3)
         load_d(4)
         load_w8s(nc.sync, 1)
         load_w8(1)
+        nc.sync.dma_start(out=up[:].bitcast(I32), in_=up_words[0].bitcast(I32))
         load_w4s(nc.sync, 1)
         load_w4(1)
         load_ups(nc.sync)
-        nc.sync.dma_start(out=up[:].bitcast(I32), in_=up_words[0].bitcast(I32))
-        load_w4s(nc.sync, 2)
         load_w8(2)
         load_w4(2)
 
@@ -179,14 +181,13 @@ def tile_mix_three_fm_bias_kernel(
 
         def y_pass(n, g, t0=0, t1=T):
             s, c = where(n)
+            ss, cc = (0, P * n) if s == 0 else (1, P * n - 512)
             if g < NO:
-                sc = w8s[0] if s == 0 else w8s[1]
-                cc = P * n if s == 0 else P * n - 512
                 lhsT = w8[s][:, g, c : c + P].bitcast(E4M3)
-                lscale = sc[4 * g : P, cc : cc + P]
+                lscale = w8s[ss][4 * g : P, cc : cc + P]
             else:
                 lhsT = w4[s][:, g - NO, 2 * c : 2 * (c + P)].bitcast(E2M1)
-                lscale = w4s[s][:, g - NO, c : c + P]
+                lscale = w4s[ss][:, g - NO, cc : cc + P]
             nc.tensor.matmul_mx(
                 out=y_acc[n][:], lhsT=lhsT, lhsT_scale=lscale,
                 rhs=x_codes[g][:, t0:t1].bitcast(E4M3), rhs_scale=x_scale[g][:, t0:t1],
@@ -226,12 +227,14 @@ def tile_mix_three_fm_bias_kernel(
             quant_d(g, d_grp, 0, 4)
             for j in range(PACK):
                 h_pass(g, j)
-        quant_x(3)
         for n in range(4):
             open_bank(n)
-        for g in range(4):
+        for g in range(3):
             for n in range(4):
                 y_pass(n, g)
+        quant_x(3)
+        for n in range(4):
+            y_pass(n, 3)
         quant_x(4)
         for n in range(4):
             y_pass(n, 4)

@@ -44,7 +44,7 @@ def tile_mix_three_fm_bias_kernel(
         d_scale = [keep.tile([P, R], U8, name=f"d_scale{g}", align_bytes=64) for g in range(NK)]
         w8 = [keep.tile([P, NO, c1 - c0], U32, name=f"w8_{c0}", align_bytes=64) for c0, c1 in SECTIONS]
         w4 = [keep.tile([P, NK - NO, 2 * (c1 - c0)], U8, name=f"w4_{c0}", align_bytes=64) for c0, c1 in SECTIONS]
-        w8s = [keep.tile([P, c1 - c0], U8, name=f"w8s_{c0}", align_bytes=64) for c0, c1 in ((0, 512), (512, 2048))]
+        w8s = keep.tile([P, M], U8, name="w8s", align_bytes=64)
         w4s = [keep.tile([P, NK - NO, c1 - c0], U8, name=f"w4s_{c0}", align_bytes=64) for c0, c1 in ((0, 512), (512, 2048))]
         up = keep.tile([P, 2 * M], U8, name="up", align_bytes=64)
         ups = keep.tile([P, M], U8, name="ups", align_bytes=64)
@@ -58,14 +58,14 @@ def tile_mix_three_fm_bias_kernel(
         h_scale = keep.tile([P, T], U8, name="h_scale", align_bytes=64)
 
         nc.vector.memset(warm[:], 0.0)
-        for t in (w8s[0], w4s[0]):
+        for t in (w8s, w4s[0]):
             flat = t[:] if len(t.shape) == 2 else t[:].rearrange("p a n -> p (a n)")
             nc.vector.memset(flat.bitcast(I32), 0)
         nc.gpsimd.memset(b_rows[:], 0.0)
         make_identity(nc, ident[:])
         nc.scalar.activation(out=warm[:], in_=warm[:], func=IDENT)
         nc.scalar.dma_start(out=b_rows[0:NT, :], in_=b.rearrange("(g p) -> g p", p=P))
-        for t in (w8s[1], w4s[1], ups):
+        for t in (w4s[1], ups):
             flat = t[:] if len(t.shape) == 2 else t[:].rearrange("p a n -> p (a n)")
             nc.vector.memset(flat.bitcast(I32), 0)
 
@@ -93,12 +93,11 @@ def tile_mix_three_fm_bias_kernel(
             c0, c1 = SECTIONS[s]
             nc.sync.dma_start(out=w4[s][:].bitcast(I32), in_=w4_view[:, :, 2 * c0 : 2 * c1].bitcast(I32))
 
-        def load_w8s(eng, s, quads=(0, 1, 2, 3)):
-            c0, c1 = ((0, 512), (512, 2048))[s]
-            for q in quads:
+        def load_w8s(eng):
+            for q in range(4):
                 eng.dma_start(
-                    out=w8s[s][32 * q : 32 * q + 8, :].bitcast(I32),
-                    in_=w8_scales[:, 4 * q : 4 * q + 4, c0:c1].bitcast(I32),
+                    out=w8s[32 * q + 4 : 32 * q + 12, :].bitcast(I32),
+                    in_=w8_scales[:, 4 * q : 4 * q + 4, :].bitcast(I32),
                 )
 
         def load_w4s(eng, s, quads=(0, 1, 2, 3)):
@@ -116,10 +115,10 @@ def tile_mix_three_fm_bias_kernel(
                     in_=up_scales[0, 4 * q : 4 * q + 4, :].bitcast(I32),
                 )
 
+        load_w8s(nc.gpsimd)
         load_x(0)
         load_d(0)
         for g in (1, 2):
-            load_w8s(nc.sync, 0, (2 * g - 2, 2 * g - 1))
             load_x(g)
             load_w4s(nc.sync, 0, (2 * g - 2, 2 * g - 1))
             load_d(g)
@@ -129,11 +128,10 @@ def tile_mix_three_fm_bias_kernel(
         load_x(4)
         load_d(3)
         load_d(4)
-        load_w8s(nc.sync, 1)
         load_w8(1)
-        nc.sync.dma_start(out=up[:].bitcast(I32), in_=up_words[0].bitcast(I32))
         load_w4s(nc.sync, 1)
         load_w4(1)
+        nc.sync.dma_start(out=up[:].bitcast(I32), in_=up_words[0].bitcast(I32))
         load_ups(nc.sync)
         load_w8(2)
         load_w4(2)
@@ -184,7 +182,7 @@ def tile_mix_three_fm_bias_kernel(
             ss, cc = (0, P * n) if s == 0 else (1, P * n - 512)
             if g < NO:
                 lhsT = w8[s][:, g, c : c + P].bitcast(E4M3)
-                lscale = w8s[ss][4 * g : P, cc : cc + P]
+                lscale = w8s[4 + 4 * g : P, P * n : P * (n + 1)]
             else:
                 lhsT = w4[s][:, g - NO, 2 * c : 2 * (c + P)].bitcast(E2M1)
                 lscale = w4s[ss][:, g - NO, cc : cc + P]
@@ -244,12 +242,7 @@ def tile_mix_three_fm_bias_kernel(
         for j in range(PACK):
             h_pass(3, j)
         d_grp = group.tile([P, PACK, P, PACK], BF16, name="d_grp", align_bytes=64)
-        for j in range(PACK):
-            copy = nc.vector.tensor_copy if j < 2 else nc.scalar.copy
-            copy(
-                out=d_grp[:, j, :, :],
-                in_=d_raw[4][:].rearrange("p j (m t) -> p m t j", t=4)[:, :, j, :],
-            )
+        spread_d(4, d_grp, 0, P)
         for j in range(PACK):
             quant_d(4, d_grp, j, j + 1)
         for j in range(PACK):

@@ -22,7 +22,7 @@ NK = K // KP
 NO = O // KP
 NT = M // P
 SECTIONS = ((0, 512), (512, 1024), (1024, 2048))
-XV = 384
+XV = 256
 
 
 def tile_mix_three_fm_bias_kernel(
@@ -150,8 +150,8 @@ def tile_mix_three_fm_bias_kernel(
         def spread_d(g, grp, m0, m1):
             for copy, j0, j1 in ((nc.vector.tensor_copy, 0, 2), (nc.scalar.copy, 2, 4)):
                 copy(
-                    out=grp[:, j0:j1, m0:m1, :].rearrange("p t m j -> p m t j"),
-                    in_=d_raw[g][:].rearrange("p j (m t) -> p m t j", t=4)[:, m0:m1, j0:j1, :],
+                    out=grp[:, j0:j1, m0:m1, :].rearrange("p t m j -> p m j t"),
+                    in_=d_raw[g][:].rearrange("p j (m t) -> p m j t", t=4)[:, m0:m1, :, j0:j1],
                 )
 
         def quant_d(g, grp, j0, j1):
@@ -248,7 +248,7 @@ def tile_mix_three_fm_bias_kernel(
         for j in range(PACK):
             h_pass(4, j)
         for j in range(PACK):
-            copy = nc.vector.tensor_copy if j % 2 == 0 else nc.scalar.copy
+            copy = nc.scalar.copy if j % 2 == 0 else nc.vector.tensor_copy
             copy(out=h_rows[:, j, :], in_=h_acc[j][:])
         for n in range(4, 8):
             open_bank(n)
@@ -260,16 +260,10 @@ def tile_mix_three_fm_bias_kernel(
         nc.vector.quantize_mx(
             out=h_codes[:].bitcast(E4M3), scales=h_scale[:], in_=h_grp[:].rearrange("p t j -> p (t j)")
         )
-        for n in (4, 5):
-            for g in range(NO, NK):
-                y_pass(n, g)
-        for n in range(4):
-            up_pass(n)
-            finish(n)
-        for n in (6, 7):
-            for g in range(NO, NK):
-                y_pass(n, g)
         for n in range(4, 8):
+            for g in range(NO, NK):
+                y_pass(n, g)
+        for n in range(8):
             up_pass(n)
             finish(n)
         for n in range(8, NT - 1):

from contextlib import ExitStack

import concourse.mybir as mybir
from concourse.masks import make_identity

O, K, R, M, T = 1024, 2560, 512, 2048, 512
FLOPS = 2 * K * R * T + 2 * (K + R) * M * T

F32 = mybir.dt.float32
BF16 = mybir.dt.bfloat16
I32 = mybir.dt.int32
U32 = mybir.dt.uint32
U8 = mybir.dt.uint8
E4M3 = mybir.dt.float8_e4m3fn_x4
E2M1 = mybir.dt.float4_e2m1fn_x4
IDENT = mybir.ActivationFunctionType.Identity

P = 128
PACK = 4
KP = 512
NK = K // KP
NO = O // KP
NT = M // P
SECTIONS = ((0, 512), (512, 1024), (1024, 2048))
XV = 256


def tile_mix_three_fm_bias_kernel(
    tc, x, w8_words, w8_scales, w4_words, w4_scales, down, up_words, up_scales, b, out
):
    nc = tc.nc
    with ExitStack() as ctx:
        keep = ctx.enter_context(tc.tile_pool(name="keep", bufs=1))
        group = ctx.enter_context(tc.tile_pool(name="group", bufs=2))
        res = ctx.enter_context(tc.tile_pool(name="res", bufs=4))
        psum = ctx.enter_context(tc.psum_pool(name="psum", bufs=1))
        ctx.enter_context(tc.manual_schedule())

        x_raw = [keep.tile([P, PACK, T], F32, name=f"x_raw{g}") for g in range(NK)]
        d_raw = [keep.tile([P, PACK, R], F32, name=f"d_raw{g}") for g in range(NK)]
        x_codes = [keep.tile([P, T], U32, name=f"x_codes{g}", align_bytes=64) for g in range(NK)]
        x_scale = [keep.tile([P, T], U8, name=f"x_scale{g}", align_bytes=64) for g in range(NK)]
        d_codes = [keep.tile([P, R], U32, name=f"d_codes{g}", align_bytes=64) for g in range(NK)]
        d_scale = [keep.tile([P, R], U8, name=f"d_scale{g}", align_bytes=64) for g in range(NK)]
        w8 = [keep.tile([P, NO, c1 - c0], U32, name=f"w8_{c0}", align_bytes=64) for c0, c1 in SECTIONS]
        w4 = [keep.tile([P, NK - NO, 2 * (c1 - c0)], U8, name=f"w4_{c0}", align_bytes=64) for c0, c1 in SECTIONS]
        w8s = keep.tile([P, M], U8, name="w8s", align_bytes=64)
        w4s = [keep.tile([P, NK - NO, c1 - c0], U8, name=f"w4s_{c0}", align_bytes=64) for c0, c1 in ((0, 512), (512, 2048))]
        up = keep.tile([P, 2 * M], U8, name="up", align_bytes=64)
        ups = keep.tile([P, M], U8, name="ups", align_bytes=64)
        b_rows = keep.tile([P, P], F32, name="b_rows")
        ident = keep.tile([P, P], F32, name="ident")
        b_col = keep.tile([P, NT], F32, name="b_col")
        warm = keep.tile([P, 1], F32, name="warm")
        h_rows = keep.tile([P, PACK, T], BF16, name="h_rows", align_bytes=64)
        h_grp = keep.tile([P, T, PACK], BF16, name="h_grp", align_bytes=64)
        h_codes = keep.tile([P, T], U32, name="h_codes", align_bytes=64)
        h_scale = keep.tile([P, T], U8, name="h_scale", align_bytes=64)

        nc.vector.memset(warm[:], 0.0)
        for t in (w8s, w4s[0]):
            flat = t[:] if len(t.shape) == 2 else t[:].rearrange("p a n -> p (a n)")
            nc.vector.memset(flat.bitcast(I32), 0)
        nc.gpsimd.memset(b_rows[:], 0.0)
        make_identity(nc, ident[:])
        nc.scalar.activation(out=warm[:], in_=warm[:], func=IDENT)
        nc.scalar.dma_start(out=b_rows[0:NT, :], in_=b.rearrange("(g p) -> g p", p=P))
        for t in (w4s[1], ups):
            flat = t[:] if len(t.shape) == 2 else t[:].rearrange("p a n -> p (a n)")
            nc.vector.memset(flat.bitcast(I32), 0)

        w8_view = w8_words.rearrange("a p n i -> p a (n i)")
        w4_view = w4_words.rearrange("a p n -> p a n")
        w4s_view = w4_scales.rearrange("a q n -> q a n")

        def load_x(g):
            nc.sync.dma_start(
                out=x_raw[g][:].rearrange("p j t -> p (j t)"),
                in_=x[KP * g : KP * (g + 1), :].rearrange("(p j) t -> p (j t)", j=PACK),
            )

        def load_d(g):
            nc.sync.dma_start(
                out=d_raw[g][:].rearrange("p j r -> p (j r)"),
                in_=down[KP * g : KP * (g + 1), :].rearrange("(p j) r -> p (j r)", j=PACK),
            )

        def load_w8(s):
            c0, c1 = SECTIONS[s]
            nc.sync.dma_start(out=w8[s][:].bitcast(I32), in_=w8_view[:, :, 4 * c0 : 4 * c1].bitcast(I32))

        def load_w4(s):
            c0, c1 = SECTIONS[s]
            nc.sync.dma_start(out=w4[s][:].bitcast(I32), in_=w4_view[:, :, 2 * c0 : 2 * c1].bitcast(I32))

        def load_w8s(eng):
            for q in range(4):
                eng.dma_start(
                    out=w8s[32 * q + 4 : 32 * q + 12, :].bitcast(I32),
                    in_=w8_scales[:, 4 * q : 4 * q + 4, :].bitcast(I32),
                )

        def load_w4s(eng, s, quads=(0, 1, 2, 3)):
            c0, c1 = ((0, 512), (512, 2048))[s]
            for q in quads:
                eng.dma_start(
                    out=w4s[s][32 * q : 32 * q + 4, :, :].bitcast(I32),
                    in_=w4s_view[4 * q : 4 * q + 4, :, c0:c1].bitcast(I32),
                )

        def load_ups(eng):
            for q in range(4):
                eng.dma_start(
                    out=ups[32 * q : 32 * q + 4, :].bitcast(I32),
                    in_=up_scales[0, 4 * q : 4 * q + 4, :].bitcast(I32),
                )

        load_w8s(nc.gpsimd)
        load_x(0)
        load_d(0)
        for g in (1, 2):
            load_x(g)
            load_w4s(nc.sync, 0, (2 * g - 2, 2 * g - 1))
            load_d(g)
        load_w8(0)
        load_w4(0)
        load_x(3)
        load_x(4)
        load_d(3)
        load_d(4)
        load_w8(1)
        load_w4s(nc.sync, 1)
        load_w4(1)
        nc.sync.dma_start(out=up[:].bitcast(I32), in_=up_words[0].bitcast(I32))
        load_ups(nc.sync)
        load_w8(2)
        load_w4(2)

        def quant_x(g):
            grp = group.tile([P, T, PACK], BF16, name="x_grp", align_bytes=64)
            for copy, c0, c1 in ((nc.vector.tensor_copy, 0, XV), (nc.scalar.copy, XV, T)):
                copy(
                    out=grp[:, c0:c1, :].rearrange("p (c i) j -> p c j i", i=4),
                    in_=x_raw[g][:, :, c0:c1].rearrange("p j (c i) -> p c j i", i=4),
                )
            nc.vector.quantize_mx(
                out=x_codes[g][:].bitcast(E4M3), scales=x_scale[g][:], in_=grp[:].rearrange("p t j -> p (t j)")
            )

        def spread_d(g, grp, m0, m1):
            for copy, j0, j1 in ((nc.vector.tensor_copy, 0, 2), (nc.scalar.copy, 2, 4)):
                copy(
                    out=grp[:, j0:j1, m0:m1, :].rearrange("p t m j -> p m j t"),
                    in_=d_raw[g][:].rearrange("p j (m t) -> p m j t", t=4)[:, m0:m1, :, j0:j1],
                )

        def quant_d(g, grp, j0, j1):
            nc.vector.quantize_mx(
                out=d_codes[g][:, P * j0 : P * j1].bitcast(E4M3),
                scales=d_scale[g][:, P * j0 : P * j1],
                in_=grp[:, j0:j1, :, :].rearrange("p t m j -> p (t m j)"),
            )

        def h_pass(g, j):
            nc.tensor.matmul_mx(
                out=h_acc[j][:],
                lhsT=d_codes[g][:, P * j : P * (j + 1)].bitcast(E4M3),
                lhsT_scale=d_scale[g][:, P * j : P * (j + 1)],
                rhs=x_codes[g][:].bitcast(E4M3),
                rhs_scale=x_scale[g][:],
                start=(g == 0),
                stop=(g == NK - 1),
            )

        def where(n):
            c = P * n
            s = 0 if c < 512 else (1 if c < 1024 else 2)
            return s, c - SECTIONS[s][0]

        def y_pass(n, g, t0=0, t1=T):
            s, c = where(n)
            ss, cc = (0, P * n) if s == 0 else (1, P * n - 512)
            if g < NO:
                lhsT = w8[s][:, g, c : c + P].bitcast(E4M3)
                lscale = w8s[4 + 4 * g : P, P * n : P * (n + 1)]
            else:
                lhsT = w4[s][:, g - NO, 2 * c : 2 * (c + P)].bitcast(E2M1)
                lscale = w4s[ss][:, g - NO, cc : cc + P]
            nc.tensor.matmul_mx(
                out=y_acc[n][:], lhsT=lhsT, lhsT_scale=lscale,
                rhs=x_codes[g][:, t0:t1].bitcast(E4M3), rhs_scale=x_scale[g][:, t0:t1],
                start=(g == 0), stop=False,
            )

        def up_pass(n, t0=0, t1=T):
            nc.tensor.matmul_mx(
                out=y_acc[n][:],
                lhsT=up[:, 2 * P * n : 2 * P * (n + 1)].bitcast(E2M1), lhsT_scale=ups[:, P * n : P * (n + 1)],
                rhs=h_codes[:, t0:t1].bitcast(E4M3), rhs_scale=h_scale[:, t0:t1],
                start=False, stop=True,
            )

        def finish(n):
            o = res.tile([P, T], F32, name="o")
            if n % 2 == 0:
                nc.scalar.activation(out=o[:], in_=y_acc[n][:], func=IDENT, bias=b_col[:, n : n + 1])
            else:
                nc.vector.tensor_scalar_add(o[:], y_acc[n][:], b_col[:, n : n + 1])
            nc.sync.dma_start(out=out[P * n : P * (n + 1), :], in_=o[:])

        y_acc = {}

        def open_bank(n):
            y_acc[n] = psum.tile([P, T], F32, name=f"bank{n % 8}")

        b_turn = psum.tile([P, P], F32, name="bank0")
        nc.tensor.transpose(b_turn[:], b_rows[:], ident[:])
        h_acc = [psum.tile([P, T], F32, name=f"bank{4 + j}") for j in range(PACK)]
        for g in range(3):
            quant_x(g)
            if g == 0:
                nc.scalar.copy(out=b_col[:], in_=b_turn[:, 0:NT])
            d_grp = group.tile([P, PACK, P, PACK], BF16, name="d_grp", align_bytes=64)
            spread_d(g, d_grp, 0, P)
            quant_d(g, d_grp, 0, 4)
            for j in range(PACK):
                h_pass(g, j)
        for n in range(4):
            open_bank(n)
        for g in range(3):
            for n in range(4):
                y_pass(n, g)
        quant_x(3)
        for n in range(4):
            y_pass(n, 3)
        quant_x(4)
        for n in range(4):
            y_pass(n, 4)
        d_grp = group.tile([P, PACK, P, PACK], BF16, name="d_grp", align_bytes=64)
        spread_d(3, d_grp, 0, P)
        quant_d(3, d_grp, 0, 4)
        for j in range(PACK):
            h_pass(3, j)
        d_grp = group.tile([P, PACK, P, PACK], BF16, name="d_grp", align_bytes=64)
        spread_d(4, d_grp, 0, P)
        for j in range(PACK):
            quant_d(4, d_grp, j, j + 1)
        for j in range(PACK):
            h_pass(4, j)
        for j in range(PACK):
            copy = nc.scalar.copy if j % 2 == 0 else nc.vector.tensor_copy
            copy(out=h_rows[:, j, :], in_=h_acc[j][:])
        for n in range(4, 8):
            open_bank(n)
        for g in range(NO):
            for n in range(4, 8):
                y_pass(n, g)
        for copy, c0, c1 in ((nc.vector.tensor_copy, 0, 320), (nc.scalar.copy, 320, T)):
            copy(out=h_grp[:, c0:c1, :], in_=h_rows[:, :, c0:c1].rearrange("p j t -> p t j"))
        nc.vector.quantize_mx(
            out=h_codes[:].bitcast(E4M3), scales=h_scale[:], in_=h_grp[:].rearrange("p t j -> p (t j)")
        )
        for n in range(4, 8):
            for g in range(NO, NK):
                y_pass(n, g)
        for n in range(8):
            up_pass(n)
            finish(n)
        for n in range(8, NT - 1):
            open_bank(n)
            for g in range(NK):
                y_pass(n, g)
            up_pass(n)
            finish(n)
        n = NT - 1
        o = res.tile([P, T], F32, name="o")
        for q in range(4):
            y_acc[n] = psum.tile([P, P], F32, name=f"bank{q}")
            for g in range(NK):
                y_pass(n, g, P * q, P * (q + 1))
            up_pass(n, P * q, P * (q + 1))
            t0, t1 = P * q, P * (q + 1)
            if q % 2 == 1:
                nc.scalar.activation(out=o[:, t0:t1], in_=y_acc[n][:], func=IDENT, bias=b_col[:, n : n + 1])
            else:
                nc.vector.tensor_scalar_add(o[:, t0:t1], y_acc[n][:], b_col[:, n : n + 1])
            if q > 0:
                s0 = 0 if q == 1 else t0
                nc.sync.dma_start(out=out[P * n : P * (n + 1), s0:t1], in_=o[:, s0:t1])
